import numpy as np
import ml_dtypes


def mxq(x, axis, fmt="e4m3"):
    dtype, down = {"e4m3": (ml_dtypes.float8_e4m3fn, 7), "e5m2": (ml_dtypes.float8_e5m2, 14)}[fmt]
    v = np.moveaxis(np.asarray(x, np.float32).astype(ml_dtypes.bfloat16).astype(np.float64), axis, -1)
    blocks = v.reshape(v.shape[:-1] + (-1, 32))
    amax = np.abs(blocks).max(-1, keepdims=True)
    byte = np.maximum(np.where(amax > 0, np.frexp(amax)[1] - 1 + 127, 0) - down, 1)
    scale = np.exp2(byte - 127.0)
    codes = (blocks / scale).astype(np.float32).astype(dtype).astype(np.float64)
    return np.moveaxis((codes * scale).reshape(v.shape), -1, axis)


WIDE = False


def mx_kscale(k):
    if not WIDE:
        return np.ones(k)
    levels = np.array([10, -10, 5, -5, 0])
    if k % 512:
        return np.exp2(np.random.permutation(np.resize(levels, k // 32))).repeat(32)
    a = np.empty((k // 512, 16))
    for p in range(k // 512):
        a[p, :8] = np.random.permutation(np.resize(levels, 8))
        for g in range(8):
            far = levels[np.abs(levels - a[p, g]) >= 10]
            a[p, g + 8] = far[np.random.randint(len(far))]
    return np.exp2(a.ravel()).repeat(32)


def f64(x):
    return np.asarray(x).astype(np.float64)


def striped8(idx):
    return np.asarray(idx).reshape(8, -1, 16).transpose(0, 2, 1).reshape(128, -1).astype(np.uint16)


def unstriped8(offs):
    return offs.reshape(8, 16, -1).transpose(0, 2, 1).reshape(8, -1).astype(np.int64)


def pick8(x, idx, run):
    r = np.arange(len(x))
    return x[r[:, None], idx[r % (8 * run) // run]]


E2M1 = np.array([0.0, 0.5, 1.0, 1.5, 2.0, 3.0, 4.0, 6.0, -0.0, -0.5, -1.0, -1.5, -2.0, -3.0, -4.0, -6.0])


def pack_weight(w, fmt):
    k, n = w.shape
    w = f64(np.asarray(w, np.float32).astype(ml_dtypes.bfloat16)).reshape(k // 32, 32, n)
    amax = np.abs(w).max(1)
    if fmt == "e4m3":
        byte = np.frexp(amax)[1] - 1 + 127 - 7
    else:
        mant, ex = np.frexp(amax / 6.0)
        byte = np.where(mant > 0.5, ex, ex - 1) + 127
    byte = np.clip(np.where(amax > 0, byte, 1), 1, 254)
    scaled = (w * np.exp2(127.0 - byte)[:, None, :]).reshape(k, n).astype(np.float32)
    by_word = np.ascontiguousarray(scaled.reshape(k // 512, 128, 4, n).transpose(0, 1, 3, 2))
    if fmt == "e4m3":
        words = by_word.astype(ml_dtypes.float8_e4m3fn).view(np.uint8)
    else:
        c = by_word.astype(ml_dtypes.float4_e2m1fn).view(np.uint8) & 0xF
        words = (c[..., 0::2] | (c[..., 1::2] << 4)).reshape(k // 512, 128, 2 * n)
    return np.ascontiguousarray(words), np.ascontiguousarray(byte.astype(np.uint8).reshape(k // 512, 16, n))


def unpack_weight(words, scales, fmt):
    g, _, n = scales.shape
    words = np.ascontiguousarray(words).reshape(g, 128, n, -1)
    if fmt == "e4m3":
        vals = words.view(ml_dtypes.float8_e4m3fn).astype(np.float64)
    else:
        nib = np.empty((g, 128, n, 4), np.uint8)
        nib[..., 0::2] = words & 0xF
        nib[..., 1::2] = words >> 4
        vals = E2M1[nib]
    vals = vals * np.repeat(np.exp2(scales.astype(np.float64) - 127.0), 8, axis=1)[..., None]
    return vals.transpose(0, 1, 3, 2).reshape(g * 512, n)


def sigmoid(v):
    return 1.0 / (1.0 + np.exp(-v))


D, K, T, I, Q = 512, 512, 1024, 512, 128


def setup_inputs():
    n = np.random.standard_normal
    idx = np.stack([np.random.permutation(T)[:I] for _ in range(8)])
    idx2 = np.stack([np.random.permutation(T)[:I] for _ in range(8)])
    idx3 = np.stack([np.random.permutation(T)[:I] for _ in range(8)])
    fd = mx_kscale(D)
    fk = mx_kscale(K)
    wqp = pack_weight(n((D, K)) * 1.0 / np.sqrt(D) * fd[:, None] * fk, "e4m3")
    keysp = pack_weight(n((K, T)) * 1.0 / np.sqrt(K) / fk[:, None], "e2m1")
    tagsp = pack_weight(n((D, T)) * 0.5 / np.sqrt(D) * fd[:, None], "e4m3")
    return {
        "states": (n((D, Q)) * 0.95 / fd[:, None]).astype(np.float32),
        "wq_words": wqp[0],
        "wq_scales": wqp[1],
        "keys_words": keysp[0],
        "keys_scales": keysp[1],
        "tags_words": tagsp[0],
        "tags_scales": tagsp[1],
        "thr": (np.random.uniform(-0.6, 0.6, (Q, 1))).astype(np.float32),
        "slope": (np.random.uniform(1.0, 3.0, (Q, 1))).astype(np.float32),
        "offs": striped8(idx),
        "offs2": striped8(idx2),
        "offs3": striped8(idx3),
    }


def reference(states, wq_words, wq_scales, keys_words, keys_scales, tags_words, tags_scales, thr, slope, offs, offs2, offs3):
    idx = unstriped8(offs)
    idx2 = unstriped8(offs2)
    idx3 = unstriped8(offs3)
    wqu = unpack_weight(wq_words, wq_scales, "e4m3")
    keysu = unpack_weight(keys_words, keys_scales, "e2m1")
    tagsu = unpack_weight(tags_words, tags_scales, "e4m3")
    statesq = mxq(f64(states), 0, "e4m3")
    qv = wqu.T @ statesq
    qvq = mxq(qv, 0, "e4m3")
    a = qvq.T @ keysu + statesq.T @ tagsu
    s1 = sigmoid(pick8(a, idx, 16) * f64(slope) + f64(thr))
    f1 = np.zeros((Q, T))
    f1[np.arange(Q)[:, None], idx2[np.arange(Q) % 128 // 16]] = s1
    cc = a + f1 * 2.0
    y = pick8(cc, idx3, 16)
    return y

@@ -1,0 +1,177 @@
+from contextlib import ExitStack
+
+import concourse.mybir as mybir
+
+D, K, T, I, Q = 512, 512, 1024, 512, 128
+FLOPS = 2 * Q * (D * K + K * T + D * T)
+
+F32 = mybir.dt.float32
+BF16 = mybir.dt.bfloat16
+I32 = mybir.dt.int32
+U32 = mybir.dt.uint32
+U16 = mybir.dt.uint16
+U8 = mybir.dt.uint8
+FP8X4 = mybir.dt.float8_e4m3fn_x4
+FP4X4 = mybir.dt.float4_e2m1fn_x4
+ACT = mybir.ActivationFunctionType
+ALU = mybir.AluOpType
+
+P = 128
+PACK = 4
+N_TILE = 256
+HALF = I // 2
+HALF_COLS = HALF // 16
+
+
+def load_scale_rows(queue, plane, scales, r):
+    rows = scales[0].rearrange("(g r) c -> r g c", r=PACK)
+    queue.dma_start(out=plane[:].bitcast(I32)[r:P:32, :], in_=rows[r].bitcast(I32))
+
+
+def tile_attend_openings_madeparts_kernel(
+    tc, states, wq_words, wq_scales, keys_words, keys_scales, tags_words, tags_scales, thr, slope, offs, offs2, offs3, out
+):
+    nc = tc.nc
+    with ExitStack() as ctx:
+        sb = ctx.enter_context(tc.tile_pool(name="sb", bufs=1))
+        psum = ctx.enter_context(tc.psum_pool(name="psum", bufs=1))
+
+        gate_list = sb.tile([P, I // 16], U16, name="gate_list")
+        place_list = sb.tile([P, I // 16], U16, name="place_list")
+        pick_list = sb.tile([P, I // 16], U16, name="pick_list")
+
+        wq_plane = sb.tile([P, K], U8, name="wq_plane", align_bytes=64)
+        tags_plane = sb.tile([P, T], U8, name="tags_plane", align_bytes=64)
+        keys_plane = sb.tile([P, T], U8, name="keys_plane", align_bytes=64)
+        gates = sb.tile([P, T], F32, name="gates")
+        nc.vector.memset(wq_plane[:].bitcast(I32), 0)
+        warm_in = sb.tile([P, 1], F32, name="warm_in")
+        warm_out = sb.tile([P, 1], F32, name="warm_out")
+        nc.vector.memset(warm_in[:], 0.0)
+        nc.scalar.activation(out=warm_out[:], in_=warm_in[:], func=ACT.Sigmoid)
+        nc.vector.memset(tags_plane[:].bitcast(I32), 0)
+        nc.gpsimd.memset(keys_plane[:].bitcast(I32), 0)
+        nc.vector.memset(gates[:], 0.0)
+
+        states_raw = sb.tile([P, PACK, Q], F32, name="states_raw")
+        wq_raw = sb.tile([P, K], U32, name="wq_raw", align_bytes=64)
+        tags_codes = sb.tile([P, T], U32, name="tags_codes", align_bytes=64)
+        keys_codes = sb.tile([P, 2 * T], U8, name="keys_codes", align_bytes=64)
+        thr_col = sb.tile([P, 1], F32, name="thr_col")
+        slope_col = sb.tile([P, 1], F32, name="slope_col")
+
+        nc.sync.dma_start(out=states_raw[:], in_=states.rearrange("(p j) q -> p j q", j=PACK))
+        load_scale_rows(nc.sync, wq_plane, wq_scales, 0)
+        load_scale_rows(nc.sync, wq_plane, wq_scales, 1)
+        load_scale_rows(nc.scalar, wq_plane, wq_scales, 2)
+        load_scale_rows(nc.scalar, wq_plane, wq_scales, 3)
+        nc.sync.dma_start(out=wq_raw[:].bitcast(I32), in_=wq_words[0].rearrange("p n t -> p (n t)").bitcast(I32))
+        load_scale_rows(nc.sync, tags_plane, tags_scales, 0)
+        nc.sync.dma_start(out=tags_codes[:].bitcast(I32), in_=tags_words[0].rearrange("p n t -> p (n t)").bitcast(I32))
+        nc.sync.dma_start(out=keys_codes[:].bitcast(I32), in_=keys_words[0].bitcast(I32))
+        load_scale_rows(nc.sync, tags_plane, tags_scales, 1)
+        load_scale_rows(nc.sync, tags_plane, tags_scales, 2)
+        load_scale_rows(nc.sync, tags_plane, tags_scales, 3)
+        load_scale_rows(nc.sync, keys_plane, keys_scales, 0)
+        load_scale_rows(nc.sync, keys_plane, keys_scales, 1)
+        load_scale_rows(nc.sync, keys_plane, keys_scales, 2)
+        load_scale_rows(nc.gpsimd, keys_plane, keys_scales, 3)
+        nc.sync.dma_start(gate_list[:], offs)
+        nc.sync.dma_start(place_list[:], offs2)
+        nc.sync.dma_start(pick_list[:], offs3)
+        nc.gpsimd.dma_start(out=thr_col[:], in_=thr)
+        nc.gpsimd.dma_start(out=slope_col[:], in_=slope)
+
+        wq_dealt = sb.tile([P, K], U32, name="wq_dealt", align_bytes=64)
+        wq_dealt_plane = sb.tile([P, K], U8, name="wq_dealt_plane", align_bytes=64)
+        nc.vector.tensor_copy(
+            out=wq_dealt_plane[:].rearrange("p (t m) -> p m t", t=PACK),
+            in_=wq_plane[:].rearrange("p (m t) -> p m t", t=PACK),
+        )
+        nc.vector.tensor_copy(
+            out=wq_dealt[:].rearrange("p (t m) -> p m t", t=PACK),
+            in_=wq_raw[:].rearrange("p (m t) -> p m t", t=PACK),
+        )
+
+        states_bf = sb.tile([P, Q, PACK], BF16, name="states_bf", align_bytes=64)
+        nc.scalar.copy(out=states_bf[:], in_=states_raw[:].rearrange("p j q -> p q j"))
+        states_codes = sb.tile([P, Q], U32, name="states_codes", align_bytes=64)
+        states_plane = sb.tile([P, Q], U8, name="states_plane", align_bytes=64)
+        nc.vector.quantize_mx(
+            out=states_codes[:].bitcast(FP8X4), scales=states_plane[:], in_=states_bf[:].rearrange("p q j -> p (q j)")
+        )
+
+        qv_bank = psum.tile([P, PACK, Q], F32, name="qv_bank")
+        for t in range(PACK):
+            cols = slice(t * P, (t + 1) * P)
+            nc.tensor.matmul_mx(
+                out=qv_bank[:, t, :],
+                lhsT=wq_dealt[:, cols].bitcast(FP8X4),
+                lhsT_scale=wq_dealt_plane[:, cols],
+                rhs=states_codes[:].bitcast(FP8X4),
+                rhs_scale=states_plane[:],
+                start=True,
+                stop=True,
+            )
+
+        banks = [psum.tile([P, N_TILE], F32, name="score_bank%d" % b) for b in range(T // N_TILE)]
+        for b in range(T // N_TILE):
+            cols = slice(b * N_TILE, (b + 1) * N_TILE)
+            nc.tensor.matmul_mx(
+                out=banks[b][:],
+                lhsT=states_codes[:].bitcast(FP8X4),
+                lhsT_scale=states_plane[:],
+                rhs=tags_codes[:, cols].bitcast(FP8X4),
+                rhs_scale=tags_plane[:, cols],
+                start=True,
+                stop=False,
+            )
+
+        qv_bf = sb.tile([P, Q, PACK], BF16, name="qv_bf", align_bytes=64)
+        nc.scalar.copy(out=qv_bf[:], in_=qv_bank[:].rearrange("p t q -> p q t"))
+        qv_codes = sb.tile([P, Q], U32, name="qv_codes", align_bytes=64)
+        qv_plane = sb.tile([P, Q], U8, name="qv_plane", align_bytes=64)
+        nc.vector.quantize_mx(
+            out=qv_codes[:].bitcast(FP8X4), scales=qv_plane[:], in_=qv_bf[:].rearrange("p q t -> p (q t)")
+        )
+
+        scores = sb.tile([P, T], F32, name="scores")
+        for b in range(T // N_TILE):
+            cols = slice(b * N_TILE, (b + 1) * N_TILE)
+            nc.tensor.matmul_mx(
+                out=banks[b][:],
+                lhsT=qv_codes[:].bitcast(FP8X4),
+                lhsT_scale=qv_plane[:],
+                rhs=keys_codes[:, 2 * b * N_TILE : 2 * (b + 1) * N_TILE].bitcast(FP4X4),
+                rhs_scale=keys_plane[:, cols],
+                start=False,
+                stop=True,
+            )
+            if b % 2 == 0:
+                nc.vector.tensor_copy(out=scores[:, cols], in_=banks[b][:])
+            else:
+                nc.scalar.copy(out=scores[:, cols], in_=banks[b][:])
+
+        for h in range(2):
+            opened = sb.tile([P, HALF], F32, name="opened%d" % h)
+            list_cols = slice(h * HALF_COLS, (h + 1) * HALF_COLS)
+            nc.scalar.activation(
+                out=opened[:],
+                in_=scores[:].indirect(gate_list[:, list_cols]),
+                func=ACT.Sigmoid,
+                bias=thr_col[:],
+                scale=slope_col[:],
+            )
+            nc.vector.tensor_copy(out=gates[:].indirect(place_list[:, list_cols]), in_=opened[:])
+
+        summed = sb.tile([P, T], F32, name="summed")
+        nc.vector.scalar_tensor_tensor(
+            out=summed[:], in0=gates[:], scalar=2.0, in1=scores[:], op0=ALU.mult, op1=ALU.add
+        )
+
+        picked0 = sb.tile([P, HALF], F32, name="picked0")
+        picked1 = sb.tile([P, HALF], F32, name="picked1")
+        nc.vector.tensor_copy(out=picked0[:], in_=summed[:].indirect(pick_list[:, 0:HALF_COLS]))
+        nc.sync.dma_start(out=out[:, 0:HALF], in_=picked0[:])
+        nc.scalar.activation(out=picked1[:], in_=summed[:].indirect(pick_list[:, HALF_COLS : 2 * HALF_COLS]), func=ACT.Copy)
+        nc.scalar.dma_start(out=out[:, HALF:I], in_=picked1[:])

@@ -19,13 +19,20 @@ ALU = mybir.AluOpType
 P = 128
 PACK = 4
 N_TILE = 256
+TAGS_ROW = 4
+WQ_ROW = 12
 HALF = I // 2
 HALF_COLS = HALF // 16
 
 
-def load_scale_rows(queue, plane, scales, r):
+def load_scale_rows(queue, plane, scales, r, first_row):
     rows = scales[0].rearrange("(g r) c -> r g c", r=PACK)
-    queue.dma_start(out=plane[:].bitcast(I32)[r:P:32, :], in_=rows[r].bitcast(I32))
+    queue.dma_start(out=plane[:].bitcast(I32)[first_row + r : P : 32, :], in_=rows[r].bitcast(I32))
+
+
+def load_tag_scale_rows(queue, plane, scales, g):
+    rows = scales[0].rearrange("(g r) (h c) -> g h r c", r=PACK, h=2)
+    queue.dma_start(out=plane[:].bitcast(I32)[32 * g + TAGS_ROW : 32 * g + TAGS_ROW + 8, :], in_=rows[g].bitcast(I32))
 
 
 def tile_attend_openings_madeparts_kernel(
@@ -41,7 +48,7 @@ def tile_attend_openings_madeparts_kernel(
         pick_list = sb.tile([P, I // 16], U16, name="pick_list")
 
         wq_plane = sb.tile([P, K], U8, name="wq_plane", align_bytes=64)
-        tags_plane = sb.tile([P, T], U8, name="tags_plane", align_bytes=64)
+        tags_plane = sb.tile([P, T // 2], U8, name="tags_plane", align_bytes=64)
         keys_plane = sb.tile([P, T], U8, name="keys_plane", align_bytes=64)
         gates = sb.tile([P, T], F32, name="gates")
         nc.vector.memset(wq_plane[:].bitcast(I32), 0)
@@ -50,7 +57,7 @@ def tile_attend_openings_madeparts_kernel(
         nc.vector.memset(warm_in[:], 0.0)
         nc.scalar.activation(out=warm_out[:], in_=warm_in[:], func=ACT.Sigmoid)
         nc.vector.memset(tags_plane[:].bitcast(I32), 0)
-        nc.gpsimd.memset(keys_plane[:].bitcast(I32), 0)
+        nc.vector.memset(keys_plane[:].bitcast(I32), 0)
         nc.vector.memset(gates[:], 0.0)
 
         states_raw = sb.tile([P, PACK, Q], F32, name="states_raw")
@@ -61,40 +68,40 @@ def tile_attend_openings_madeparts_kernel(
         slope_col = sb.tile([P, 1], F32, name="slope_col")
 
         nc.sync.dma_start(out=states_raw[:], in_=states.rearrange("(p j) q -> p j q", j=PACK))
-        load_scale_rows(nc.sync, wq_plane, wq_scales, 0)
-        load_scale_rows(nc.sync, wq_plane, wq_scales, 1)
-        load_scale_rows(nc.scalar, wq_plane, wq_scales, 2)
-        load_scale_rows(nc.scalar, wq_plane, wq_scales, 3)
+        load_scale_rows(nc.sync, wq_plane, wq_scales, 0, WQ_ROW)
+        load_scale_rows(nc.sync, wq_plane, wq_scales, 1, WQ_ROW)
+        load_scale_rows(nc.scalar, wq_plane, wq_scales, 2, WQ_ROW)
+        load_scale_rows(nc.scalar, wq_plane, wq_scales, 3, WQ_ROW)
         nc.sync.dma_start(out=wq_raw[:].bitcast(I32), in_=wq_words[0].rearrange("p n t -> p (n t)").bitcast(I32))
-        load_scale_rows(nc.sync, tags_plane, tags_scales, 0)
+        load_tag_scale_rows(nc.sync, tags_plane, tags_scales, 0)
         nc.sync.dma_start(out=tags_codes[:].bitcast(I32), in_=tags_words[0].rearrange("p n t -> p (n t)").bitcast(I32))
+        load_tag_scale_rows(nc.sync, tags_plane, tags_scales, 1)
+        load_tag_scale_rows(nc.sync, tags_plane, tags_scales, 2)
+        load_tag_scale_rows(nc.sync, tags_plane, tags_scales, 3)
         nc.sync.dma_start(out=keys_codes[:].bitcast(I32), in_=keys_words[0].bitcast(I32))
-        load_scale_rows(nc.sync, tags_plane, tags_scales, 1)
-        load_scale_rows(nc.sync, tags_plane, tags_scales, 2)
-        load_scale_rows(nc.sync, tags_plane, tags_scales, 3)
-        load_scale_rows(nc.sync, keys_plane, keys_scales, 0)
-        load_scale_rows(nc.sync, keys_plane, keys_scales, 1)
-        load_scale_rows(nc.sync, keys_plane, keys_scales, 2)
-        load_scale_rows(nc.gpsimd, keys_plane, keys_scales, 3)
+        load_scale_rows(nc.sync, keys_plane, keys_scales, 0, 0)
+        load_scale_rows(nc.sync, keys_plane, keys_scales, 1, 0)
+        load_scale_rows(nc.sync, keys_plane, keys_scales, 2, 0)
+        load_scale_rows(nc.gpsimd, keys_plane, keys_scales, 3, 0)
         nc.sync.dma_start(gate_list[:], offs)
+        nc.gpsimd.dma_start(out=thr_col[:], in_=thr)
+        nc.sync.dma_start(out=slope_col[:], in_=slope)
         nc.sync.dma_start(place_list[:], offs2)
         nc.sync.dma_start(pick_list[:], offs3)
-        nc.gpsimd.dma_start(out=thr_col[:], in_=thr)
-        nc.gpsimd.dma_start(out=slope_col[:], in_=slope)
 
         wq_dealt = sb.tile([P, K], U32, name="wq_dealt", align_bytes=64)
         wq_dealt_plane = sb.tile([P, K], U8, name="wq_dealt_plane", align_bytes=64)
         nc.vector.tensor_copy(
-            out=wq_dealt_plane[:].rearrange("p (t m) -> p m t", t=PACK),
-            in_=wq_plane[:].rearrange("p (m t) -> p m t", t=PACK),
+            out=wq_dealt_plane[:].rearrange("p (t m) -> p t m", t=PACK),
+            in_=wq_plane[:].rearrange("p (m t) -> p t m", t=PACK),
         )
-        nc.vector.tensor_copy(
-            out=wq_dealt[:].rearrange("p (t m) -> p m t", t=PACK),
-            in_=wq_raw[:].rearrange("p (m t) -> p m t", t=PACK),
-        )
+        dealt_view = wq_dealt[:].rearrange("p (t c i) -> p c t i", t=PACK, i=4)
+        raw_view = wq_raw[:].rearrange("p (c i t) -> p c t i", t=PACK, i=4)
+        nc.scalar.copy(out=dealt_view[:, :, 0:2, :], in_=raw_view[:, :, 0:2, :])
+        nc.scalar.copy(out=dealt_view[:, :, 2:4, :], in_=raw_view[:, :, 2:4, :])
 
         states_bf = sb.tile([P, Q, PACK], BF16, name="states_bf", align_bytes=64)
-        nc.scalar.copy(out=states_bf[:], in_=states_raw[:].rearrange("p j q -> p q j"))
+        nc.vector.tensor_copy(out=states_bf[:], in_=states_raw[:].rearrange("p j q -> p q j"))
         states_codes = sb.tile([P, Q], U32, name="states_codes", align_bytes=64)
         states_plane = sb.tile([P, Q], U8, name="states_plane", align_bytes=64)
         nc.vector.quantize_mx(
@@ -107,7 +114,7 @@ def tile_attend_openings_madeparts_kernel(
             nc.tensor.matmul_mx(
                 out=qv_bank[:, t, :],
                 lhsT=wq_dealt[:, cols].bitcast(FP8X4),
-                lhsT_scale=wq_dealt_plane[:, cols],
+                lhsT_scale=wq_dealt_plane[WQ_ROW:P, cols],
                 rhs=states_codes[:].bitcast(FP8X4),
                 rhs_scale=states_plane[:],
                 start=True,
@@ -122,7 +129,7 @@ def tile_attend_openings_madeparts_kernel(
                 lhsT=states_codes[:].bitcast(FP8X4),
                 lhsT_scale=states_plane[:],
                 rhs=tags_codes[:, cols].bitcast(FP8X4),
-                rhs_scale=tags_plane[:, cols],
+                rhs_scale=tags_plane[TAGS_ROW + PACK * (b // 2) : P, (b % 2) * N_TILE : (b % 2 + 1) * N_TILE],
                 start=True,
                 stop=False,
             )

from contextlib import ExitStack

import concourse.mybir as mybir

D, K, T, I, Q = 512, 512, 1024, 512, 128
FLOPS = 2 * Q * (D * K + K * T + D * T)

F32 = mybir.dt.float32
BF16 = mybir.dt.bfloat16
I32 = mybir.dt.int32
U32 = mybir.dt.uint32
U16 = mybir.dt.uint16
U8 = mybir.dt.uint8
FP8X4 = mybir.dt.float8_e4m3fn_x4
FP4X4 = mybir.dt.float4_e2m1fn_x4
ACT = mybir.ActivationFunctionType
ALU = mybir.AluOpType

P = 128
PACK = 4
N_TILE = 256
TAGS_ROW = 4
WQ_ROW = 12
HALF = I // 2
HALF_COLS = HALF // 16


def load_scale_rows(queue, plane, scales, r, first_row):
    rows = scales[0].rearrange("(g r) c -> r g c", r=PACK)
    queue.dma_start(out=plane[:].bitcast(I32)[first_row + r : P : 32, :], in_=rows[r].bitcast(I32))


def load_tag_scale_rows(queue, plane, scales, g):
    rows = scales[0].rearrange("(g r) (h c) -> g h r c", r=PACK, h=2)
    queue.dma_start(out=plane[:].bitcast(I32)[32 * g + TAGS_ROW : 32 * g + TAGS_ROW + 8, :], in_=rows[g].bitcast(I32))


def tile_attend_openings_madeparts_kernel(
    tc, states, wq_words, wq_scales, keys_words, keys_scales, tags_words, tags_scales, thr, slope, offs, offs2, offs3, out
):
    nc = tc.nc
    with ExitStack() as ctx:
        sb = ctx.enter_context(tc.tile_pool(name="sb", bufs=1))
        psum = ctx.enter_context(tc.psum_pool(name="psum", bufs=1))

        gate_list = sb.tile([P, I // 16], U16, name="gate_list")
        place_list = sb.tile([P, I // 16], U16, name="place_list")
        pick_list = sb.tile([P, I // 16], U16, name="pick_list")

        wq_plane = sb.tile([P, K], U8, name="wq_plane", align_bytes=64)
        tags_plane = sb.tile([P, T // 2], U8, name="tags_plane", align_bytes=64)
        keys_plane = sb.tile([P, T], U8, name="keys_plane", align_bytes=64)
        gates = sb.tile([P, T], F32, name="gates")
        nc.vector.memset(wq_plane[:].bitcast(I32), 0)
        warm_in = sb.tile([P, 1], F32, name="warm_in")
        warm_out = sb.tile([P, 1], F32, name="warm_out")
        nc.vector.memset(warm_in[:], 0.0)
        nc.scalar.activation(out=warm_out[:], in_=warm_in[:], func=ACT.Sigmoid)
        nc.vector.memset(tags_plane[:].bitcast(I32), 0)
        nc.vector.memset(keys_plane[:].bitcast(I32), 0)
        nc.vector.memset(gates[:], 0.0)

        states_raw = sb.tile([P, PACK, Q], F32, name="states_raw")
        wq_raw = sb.tile([P, K], U32, name="wq_raw", align_bytes=64)
        tags_codes = sb.tile([P, T], U32, name="tags_codes", align_bytes=64)
        keys_codes = sb.tile([P, 2 * T], U8, name="keys_codes", align_bytes=64)
        thr_col = sb.tile([P, 1], F32, name="thr_col")
        slope_col = sb.tile([P, 1], F32, name="slope_col")

        nc.sync.dma_start(out=states_raw[:], in_=states.rearrange("(p j) q -> p j q", j=PACK))
        load_scale_rows(nc.sync, wq_plane, wq_scales, 0, WQ_ROW)
        load_scale_rows(nc.sync, wq_plane, wq_scales, 1, WQ_ROW)
        load_scale_rows(nc.scalar, wq_plane, wq_scales, 2, WQ_ROW)
        load_scale_rows(nc.scalar, wq_plane, wq_scales, 3, WQ_ROW)
        nc.sync.dma_start(out=wq_raw[:].bitcast(I32), in_=wq_words[0].rearrange("p n t -> p (n t)").bitcast(I32))
        load_tag_scale_rows(nc.sync, tags_plane, tags_scales, 0)
        nc.sync.dma_start(out=tags_codes[:].bitcast(I32), in_=tags_words[0].rearrange("p n t -> p (n t)").bitcast(I32))
        load_tag_scale_rows(nc.sync, tags_plane, tags_scales, 1)
        load_tag_scale_rows(nc.sync, tags_plane, tags_scales, 2)
        load_tag_scale_rows(nc.sync, tags_plane, tags_scales, 3)
        nc.sync.dma_start(out=keys_codes[:].bitcast(I32), in_=keys_words[0].bitcast(I32))
        load_scale_rows(nc.sync, keys_plane, keys_scales, 0, 0)
        load_scale_rows(nc.sync, keys_plane, keys_scales, 1, 0)
        load_scale_rows(nc.sync, keys_plane, keys_scales, 2, 0)
        load_scale_rows(nc.gpsimd, keys_plane, keys_scales, 3, 0)
        nc.sync.dma_start(gate_list[:], offs)
        nc.gpsimd.dma_start(out=thr_col[:], in_=thr)
        nc.sync.dma_start(out=slope_col[:], in_=slope)
        nc.sync.dma_start(place_list[:], offs2)
        nc.sync.dma_start(pick_list[:], offs3)

        wq_dealt = sb.tile([P, K], U32, name="wq_dealt", align_bytes=64)
        wq_dealt_plane = sb.tile([P, K], U8, name="wq_dealt_plane", align_bytes=64)
        nc.vector.tensor_copy(
            out=wq_dealt_plane[:].rearrange("p (t m) -> p t m", t=PACK),
            in_=wq_plane[:].rearrange("p (m t) -> p t m", t=PACK),
        )
        dealt_view = wq_dealt[:].rearrange("p (t c i) -> p c t i", t=PACK, i=4)
        raw_view = wq_raw[:].rearrange("p (c i t) -> p c t i", t=PACK, i=4)
        nc.scalar.copy(out=dealt_view[:, :, 0:2, :], in_=raw_view[:, :, 0:2, :])
        nc.scalar.copy(out=dealt_view[:, :, 2:4, :], in_=raw_view[:, :, 2:4, :])

        states_bf = sb.tile([P, Q, PACK], BF16, name="states_bf", align_bytes=64)
        nc.vector.tensor_copy(out=states_bf[:], in_=states_raw[:].rearrange("p j q -> p q j"))
        states_codes = sb.tile([P, Q], U32, name="states_codes", align_bytes=64)
        states_plane = sb.tile([P, Q], U8, name="states_plane", align_bytes=64)
        nc.vector.quantize_mx(
            out=states_codes[:].bitcast(FP8X4), scales=states_plane[:], in_=states_bf[:].rearrange("p q j -> p (q j)")
        )

        qv_bank = psum.tile([P, PACK, Q], F32, name="qv_bank")
        for t in range(PACK):
            cols = slice(t * P, (t + 1) * P)
            nc.tensor.matmul_mx(
                out=qv_bank[:, t, :],
                lhsT=wq_dealt[:, cols].bitcast(FP8X4),
                lhsT_scale=wq_dealt_plane[WQ_ROW:P, cols],
                rhs=states_codes[:].bitcast(FP8X4),
                rhs_scale=states_plane[:],
                start=True,
                stop=True,
            )

        banks = [psum.tile([P, N_TILE], F32, name="score_bank%d" % b) for b in range(T // N_TILE)]
        for b in range(T // N_TILE):
            cols = slice(b * N_TILE, (b + 1) * N_TILE)
            nc.tensor.matmul_mx(
                out=banks[b][:],
                lhsT=states_codes[:].bitcast(FP8X4),
                lhsT_scale=states_plane[:],
                rhs=tags_codes[:, cols].bitcast(FP8X4),
                rhs_scale=tags_plane[TAGS_ROW + PACK * (b // 2) : P, (b % 2) * N_TILE : (b % 2 + 1) * N_TILE],
                start=True,
                stop=False,
            )

        qv_bf = sb.tile([P, Q, PACK], BF16, name="qv_bf", align_bytes=64)
        nc.scalar.copy(out=qv_bf[:], in_=qv_bank[:].rearrange("p t q -> p q t"))
        qv_codes = sb.tile([P, Q], U32, name="qv_codes", align_bytes=64)
        qv_plane = sb.tile([P, Q], U8, name="qv_plane", align_bytes=64)
        nc.vector.quantize_mx(
            out=qv_codes[:].bitcast(FP8X4), scales=qv_plane[:], in_=qv_bf[:].rearrange("p q t -> p (q t)")
        )

        scores = sb.tile([P, T], F32, name="scores")
        for b in range(T // N_TILE):
            cols = slice(b * N_TILE, (b + 1) * N_TILE)
            nc.tensor.matmul_mx(
                out=banks[b][:],
                lhsT=qv_codes[:].bitcast(FP8X4),
                lhsT_scale=qv_plane[:],
                rhs=keys_codes[:, 2 * b * N_TILE : 2 * (b + 1) * N_TILE].bitcast(FP4X4),
                rhs_scale=keys_plane[:, cols],
                start=False,
                stop=True,
            )
            if b % 2 == 0:
                nc.vector.tensor_copy(out=scores[:, cols], in_=banks[b][:])
            else:
                nc.scalar.copy(out=scores[:, cols], in_=banks[b][:])

        for h in range(2):
            opened = sb.tile([P, HALF], F32, name="opened%d" % h)
            list_cols = slice(h * HALF_COLS, (h + 1) * HALF_COLS)
            nc.scalar.activation(
                out=opened[:],
                in_=scores[:].indirect(gate_list[:, list_cols]),
                func=ACT.Sigmoid,
                bias=thr_col[:],
                scale=slope_col[:],
            )
            nc.vector.tensor_copy(out=gates[:].indirect(place_list[:, list_cols]), in_=opened[:])

        summed = sb.tile([P, T], F32, name="summed")
        nc.vector.scalar_tensor_tensor(
            out=summed[:], in0=gates[:], scalar=2.0, in1=scores[:], op0=ALU.mult, op1=ALU.add
        )

        picked0 = sb.tile([P, HALF], F32, name="picked0")
        picked1 = sb.tile([P, HALF], F32, name="picked1")
        nc.vector.tensor_copy(out=picked0[:], in_=summed[:].indirect(pick_list[:, 0:HALF_COLS]))
        nc.sync.dma_start(out=out[:, 0:HALF], in_=picked0[:])
        nc.scalar.activation(out=picked1[:], in_=summed[:].indirect(pick_list[:, HALF_COLS : 2 * HALF_COLS]), func=ACT.Copy)
        nc.scalar.dma_start(out=out[:, HALF:I], in_=picked1[:])
